import numpy as np
import ml_dtypes


def mxq(x, axis, fmt="e4m3"):
    dtype, down = {"e4m3": (ml_dtypes.float8_e4m3fn, 7), "e5m2": (ml_dtypes.float8_e5m2, 14)}[fmt]
    v = np.moveaxis(np.asarray(x, np.float32).astype(ml_dtypes.bfloat16).astype(np.float64), axis, -1)
    blocks = v.reshape(v.shape[:-1] + (-1, 32))
    amax = np.abs(blocks).max(-1, keepdims=True)
    byte = np.maximum(np.where(amax > 0, np.frexp(amax)[1] - 1 + 127, 0) - down, 1)
    scale = np.exp2(byte - 127.0)
    codes = (blocks / scale).astype(np.float32).astype(dtype).astype(np.float64)
    return np.moveaxis((codes * scale).reshape(v.shape), -1, axis)


WIDE = False


def mx_kscale(k):
    if not WIDE:
        return np.ones(k)
    levels = np.array([10, -10, 5, -5, 0])
    if k % 512:
        return np.exp2(np.random.permutation(np.resize(levels, k // 32))).repeat(32)
    a = np.empty((k // 512, 16))
    for p in range(k // 512):
        a[p, :8] = np.random.permutation(np.resize(levels, 8))
        for g in range(8):
            far = levels[np.abs(levels - a[p, g]) >= 10]
            a[p, g + 8] = far[np.random.randint(len(far))]
    return np.exp2(a.ravel()).repeat(32)


def f64(x):
    return np.asarray(x).astype(np.float64)


def striped(idx):
    return np.tile(idx.reshape(-1, 16).T, (8, 1)).astype(np.uint16)


def unstriped(offs):
    return offs[:16].T.reshape(-1).astype(np.int64)


E2M1 = np.array([0.0, 0.5, 1.0, 1.5, 2.0, 3.0, 4.0, 6.0, -0.0, -0.5, -1.0, -1.5, -2.0, -3.0, -4.0, -6.0])


def pack_weight(w, fmt):
    k, n = w.shape
    w = f64(np.asarray(w, np.float32).astype(ml_dtypes.bfloat16)).reshape(k // 32, 32, n)
    amax = np.abs(w).max(1)
    if fmt == "e4m3":
        byte = np.frexp(amax)[1] - 1 + 127 - 7
    else:
        mant, ex = np.frexp(amax / 6.0)
        byte = np.where(mant > 0.5, ex, ex - 1) + 127
    byte = np.clip(np.where(amax > 0, byte, 1), 1, 254)
    scaled = (w * np.exp2(127.0 - byte)[:, None, :]).reshape(k, n).astype(np.float32)
    by_word = np.ascontiguousarray(scaled.reshape(k // 512, 128, 4, n).transpose(0, 1, 3, 2))
    if fmt == "e4m3":
        words = by_word.astype(ml_dtypes.float8_e4m3fn).view(np.uint8)
    else:
        c = by_word.astype(ml_dtypes.float4_e2m1fn).view(np.uint8) & 0xF
        words = (c[..., 0::2] | (c[..., 1::2] << 4)).reshape(k // 512, 128, 2 * n)
    return np.ascontiguousarray(words), np.ascontiguousarray(byte.astype(np.uint8).reshape(k // 512, 16, n))


def unpack_weight(words, scales, fmt):
    g, _, n = scales.shape
    words = np.ascontiguousarray(words).reshape(g, 128, n, -1)
    if fmt == "e4m3":
        vals = words.view(ml_dtypes.float8_e4m3fn).astype(np.float64)
    else:
        nib = np.empty((g, 128, n, 4), np.uint8)
        nib[..., 0::2] = words & 0xF
        nib[..., 1::2] = words >> 4
        vals = E2M1[nib]
    vals = vals * np.repeat(np.exp2(scales.astype(np.float64) - 127.0), 8, axis=1)[..., None]
    return vals.transpose(0, 1, 3, 2).reshape(g * 512, n)


def gelu(v):
    return 0.5 * v * (1.0 + np.tanh(np.sqrt(2.0 / np.pi) * (v + 0.044715 * v**3)))


def bf(x):
    return np.asarray(x, np.float32).astype(ml_dtypes.bfloat16)


def planes(Y):
    n, m = Y.shape
    b = f64(bf(Y)).reshape(n // 32, 32, m)
    amax = np.abs(b).max(1)
    byte = np.clip(np.where(amax > 0, np.frexp(amax)[1] - 1 + 127 - 7, 1), 1, 254)
    codes = (b * np.exp2(127.0 - byte)[:, None, :]).reshape(n, m).astype(np.float32).astype(ml_dtypes.float8_e4m3fn).view(np.uint8)
    words = codes.reshape(n // 512, 128, 4, m).transpose(0, 1, 3, 2)
    return np.ascontiguousarray(words), np.ascontiguousarray(byte.astype(np.uint8).reshape(n // 512, 16, m))


K, H, N, T, S, P = 1536, 1024, 1024, 4096, 1024, 512

def setup_inputs():
    n = np.random.standard_normal
    s = mx_kscale(K)[:, None]
    u = mx_kscale(H)[:, None]
    d = {}
    d["tab_words"], d["tab_scales"] = pack_weight(n((K, T)) * s, "e2m1")
    d["offs"] = striped(np.random.permutation(T)[:S])
    d["pos1"] = striped(np.random.permutation(S)[:P])
    d["pos2"] = striped(np.random.permutation(S)[:P])
    d["w1"] = (n((K, H)) / K ** 0.5 / s * u.T).astype(np.float32)
    d["b1"] = (0.6 * n(H) * u[:, 0]).astype(np.float32)
    d["gain"] = (0.9 * np.exp(0.3 * n(H)) / u[:, 0]).astype(np.float32)
    w4 = n((H, N)) / H ** 0.5 / u * np.exp(0.8 * n(N))[None, :]
    d["w4_words"], d["w4_scales"] = pack_weight(w4, "e2m1")
    return d

def reference(tab_words, tab_scales, offs, pos1, pos2, w1, b1, gain, w4_words, w4_scales):
    v = unpack_weight(tab_words, tab_scales, "e2m1")[:, unstriped(offs)]
    h = (mxq(f64(w1), 0, "e4m3").T @ v) + f64(b1)[:, None]
    lead = h[:, unstriped(pos1)]
    tail = f64(gain)[:, None] * h[:, unstriped(pos2)]
    z = lead / (1.0 + np.square(tail))
    zq = mxq(z, 0, "e4m3")
    w4 = unpack_weight(w4_words, w4_scales, "e2m1")
    y = w4.T @ zq
    words, scales = planes(y)
    return y, words, scales

@@ -1,0 +1,273 @@
+from contextlib import ExitStack
+
+import concourse.mybir as mybir
+
+K, H, N, T, S, M = 1536, 1024, 1024, 4096, 1024, 512
+FLOPS = 2 * K * H * S + 2 * H * N * M
+
+F32 = mybir.dt.float32
+BF16 = mybir.dt.bfloat16
+I32 = mybir.dt.int32
+U32 = mybir.dt.uint32
+U16 = mybir.dt.uint16
+U8 = mybir.dt.uint8
+FP8X4 = mybir.dt.float8_e4m3fn_x4
+FP4X4 = mybir.dt.float4_e2m1fn_x4
+ACT = mybir.ActivationFunctionType
+ALU = mybir.AluOpType
+
+P = 128
+PACK = 4
+PASS = P * PACK
+BANK = 512
+K_PASSES = K // PASS
+H_PASSES = H // PASS
+N_GROUPS = N // PASS
+QUADS = 4
+LIVE_SPAN = 100
+SCALE_ROW0 = 20
+PAIR = 2
+CHUNKS = ((0, 256), (256, 512))
+
+
+def tile_list_lead_tail_fouling_kernel(
+    tc, tab_words, tab_scales, offs, pos1, pos2, w1, b1, gain, w4_words, w4_scales, out_0, out_1, out_2
+):
+    nc = tc.nc
+    with ExitStack() as ctx:
+        keep = ctx.enter_context(tc.tile_pool(name="keep", bufs=1))
+        ring = ctx.enter_context(tc.tile_pool(name="ring", bufs=4))
+        psum = ctx.enter_context(tc.psum_pool(name="psum", bufs=1))
+
+        def held(shape, dtype, name):
+            return keep.tile(shape, dtype, name=name, align_bytes=64)
+
+        offs_sb = held([P, S // 16], U16, "offs")
+        pos1_sb = held([P, M // 16], U16, "pos1")
+        pos2_sb = held([P, M // 16], U16, "pos2")
+        tab_s = held([P, T], U8, "tab_s")
+        v_w = [held([P, S], U16, "v_w%d" % a) for a in range(K_PASSES)]
+        v_s_all = held([P, S], U8, "v_s_all")
+        v_s = [held([P, S], U8, "v_s%d" % a) for a in range(K_PASSES)]
+        w1_w = {(b, a): held([P, PASS], U32, "w1_w%d%d" % (b, a)) for b in range(H_PASSES) for a in range(K_PASSES)}
+        w1_s = {(b, a): held([P, PASS], U8, "w1_s%d%d" % (b, a)) for b in range(H_PASSES) for a in range(K_PASSES)}
+        bias = held([P, H_PASSES, PACK], F32, "bias")
+        gains = held([P, H_PASSES, PACK], F32, "gains")
+        w4_s_raw = held([P, H_PASSES * N], U8, "w4_s_raw")
+        w4_w = held([P, H_PASSES * N], U16, "w4_w")
+        w4_s = held([P, H_PASSES * N], U8, "w4_s")
+        h = {(b, t): held([P, S], F32, "h%d%d" % (b, t)) for b in range(H_PASSES) for t in range(PACK)}
+        z_w = [held([P, M], U32, "z_w%d" % b) for b in range(H_PASSES)]
+        z_s = [held([P, M], U8, "z_s%d" % b) for b in range(H_PASSES)]
+        y_s = held([P, N_GROUPS, M], U8, "y_s")
+
+        def landing(shape, dtype):
+            return ring.tile(shape, dtype, name="landing", align_bytes=64)
+
+        def load_tab(a):
+            words = landing([P, T], U16)
+            nc.sync.dma_start(out=words[:].bitcast(I32), in_=tab_words[a].bitcast(I32))
+            return words
+
+        def load_w1(b, a):
+            raw = landing([P, PACK, PASS], F32)
+            rows = w1[PASS * a : PASS * (a + 1), PASS * b : PASS * (b + 1)]
+            nc.sync.dma_start(out=raw[:], in_=rows.rearrange("(p j) c -> p j c", j=PACK))
+            return raw
+
+        def load_w4():
+            raw = landing([P, H_PASSES * N], U16)
+            nc.sync.dma_start(
+                out=raw[:].bitcast(I32).rearrange("p (a n) -> p a n", a=H_PASSES),
+                in_=w4_words.bitcast(I32).rearrange("a p n -> p a n"),
+            )
+            return raw
+
+        for a in range(K_PASSES):
+            nc.vector.memset(v_s[a][:].bitcast(I32), 0)
+        nc.gpsimd.memset(w4_s_raw[:].bitcast(I32), 0)
+        for q in range(QUADS):
+            nc.gpsimd.dma_start(
+                out=w4_s_raw[32 * q : 32 * q + 4, :].bitcast(I32).rearrange("r (a n) -> r a n", a=H_PASSES),
+                in_=w4_scales[:, 4 * q : 4 * q + 4, :].bitcast(I32).rearrange("a r n -> r a n"),
+            )
+
+        def round_w1(raw, pair, on_vector):
+            grouped = ring.tile([P, PAIR * PASS], BF16, name="w1_bf", align_bytes=64)
+            dst = grouped[:].rearrange("p (t m j) -> p m j t", t=PAIR, j=PACK)
+            src = raw[:].rearrange("p j (m t) -> p m j t", t=PACK)[:, :, :, PAIR * pair : PAIR * (pair + 1)]
+            if on_vector:
+                nc.vector.tensor_copy(dst, src)
+            else:
+                nc.scalar.activation(out=dst, in_=src, func=ACT.Copy)
+            return grouped
+
+        def quantise_w1(b, a, pair, grouped):
+            cols = slice(PAIR * P * pair, PAIR * P * (pair + 1))
+            nc.vector.quantize_mx(out=w1_w[b, a][:, cols].bitcast(FP8X4), scales=w1_s[b, a][:, cols], in_=grouped[:])
+
+        def bank(i, shape):
+            return psum.tile(shape, F32, name="bank%d" % i)
+
+        def first_pass(acc, b, t, a):
+            for s in range(S // BANK):
+                rows = slice(P * t, P * (t + 1))
+                cols = slice(BANK * s, BANK * (s + 1))
+                nc.tensor.matmul_mx(
+                    out=acc[s][:],
+                    lhsT=w1_w[b, a][:, rows].bitcast(FP8X4),
+                    lhsT_scale=w1_s[b, a][:, rows],
+                    rhs=v_w[a][:, cols].bitcast(FP4X4),
+                    rhs_scale=v_s[a][:, cols],
+                    start=(a == 0),
+                    stop=(a == K_PASSES - 1),
+                )
+
+        def leave_h(acc, b, t):
+            for s in range(S // BANK):
+                nc.scalar.activation(
+                    out=h[b, t][:, BANK * s : BANK * (s + 1)], in_=acc[s][:], func=ACT.Identity, bias=bias[:, b, t : t + 1]
+                )
+
+        tab_w = [load_tab(0)]
+        nc.sync.dma_start(offs_sb[:], offs)
+        for q in range(QUADS):
+            nc.vector.memset(tab_s[32 * q : 32 * q + SCALE_ROW0, :].bitcast(I32), 0)
+            nc.sync.dma_start(
+                out=tab_s[32 * q + SCALE_ROW0 : 32 * (q + 1), :].bitcast(I32),
+                in_=tab_scales[:, 4 * q : 4 * q + 4, :].bitcast(I32),
+            )
+        tab_w.extend(load_tab(a) for a in range(1, K_PASSES))
+        nc.vector.tensor_copy(v_s_all[:], tab_s[:].indirect(offs_sb[:]))
+        for a in range(K_PASSES):
+            row = SCALE_ROW0 + 4 * a
+            nc.scalar.dma_start(out=v_s[a][0:LIVE_SPAN, :].bitcast(I32), in_=v_s_all[row : row + LIVE_SPAN, :].bitcast(I32))
+        for a in range(K_PASSES):
+            nc.vector.tensor_copy(v_w[a][:], tab_w[a][:].indirect(offs_sb[:]))
+        acc0 = [[bank(2 * t + s, [P, BANK]) for s in range(2)] for t in range(PACK)]
+        for a in range(K_PASSES):
+            raw = load_w1(0, a)
+            halves = [round_w1(raw, pair, pair == 0) for pair in range(2)]
+            for pair in range(2):
+                quantise_w1(0, a, pair, halves[pair])
+                for t in range(PAIR * pair, PAIR * (pair + 1)):
+                    first_pass(acc0[t], 0, t, a)
+        nc.sync.dma_start(out=bias[:], in_=b1.rearrange("(b p t) -> p b t", p=P, t=PACK))
+        nc.sync.dma_start(out=gains[:], in_=gain.rearrange("(b p t) -> p b t", p=P, t=PACK))
+        nc.sync.dma_start(pos2_sb[:], pos2)
+        nc.sync.dma_start(pos1_sb[:], pos1)
+        w4_w_raw = load_w4()
+
+        def unit_tiles(b, lo, hi):
+            w = hi - lo
+            name = "%d_%d" % (b, lo)
+            return held([P, PACK, w], F32, "damp" + name), held([P, PACK, w], F32, "lead" + name)
+
+        def pick_tail(damp, b, t, lo, hi):
+            nc.vector.tensor_copy(damp[:, t, :], h[b, t][:].indirect(pos2_sb[:, lo // 16 : hi // 16]))
+
+        def root_damp(damp, b, t):
+            nc.scalar.activation(out=damp[:, t, :], in_=damp[:, t, :], func=ACT.Square, scale=gains[:, b, t : t + 1])
+            nc.scalar.activation(out=damp[:, t, :], in_=damp[:, t, :], func=ACT.Abs_reciprocal_sqrt, bias=1.0)
+
+        def pick_lead(lead, damp, b, t, lo, hi):
+            nc.vector.tensor_tensor(lead[:, t, :], h[b, t][:].indirect(pos1_sb[:, lo // 16 : hi // 16]), damp[:, t, :], ALU.mult)
+
+        def round_z(lead, damp, b, lo, hi):
+            z_bf = held([P, hi - lo, PACK], BF16, "z_bf%d_%d" % (b, lo))
+            nc.vector.tensor_tensor(
+                z_bf[:].rearrange("p (c i) t -> p c t i", i=4),
+                lead[:].rearrange("p t (c i) -> p c t i", i=4),
+                damp[:].rearrange("p t (c i) -> p c t i", i=4),
+                ALU.mult,
+            )
+            return z_bf
+
+        def quantise_z(z_bf, b, lo, hi):
+            nc.vector.quantize_mx(
+                out=z_w[b][:, lo:hi].bitcast(FP8X4), scales=z_s[b][:, lo:hi], in_=z_bf[:].rearrange("p m t -> p (m t)")
+            )
+
+        def deal_w4():
+            nc.vector.tensor_copy(
+                w4_w[:].rearrange("p (g t m) -> p g t m", t=PACK, m=P), w4_w_raw[:].rearrange("p (g m t) -> p g t m", t=PACK, m=P)
+            )
+            nc.vector.tensor_copy(
+                w4_s[:].rearrange("p (g t m) -> p g t m", t=PACK, m=P), w4_s_raw[:].rearrange("p (g m t) -> p g t m", t=PACK, m=P)
+            )
+
+        damp0, lead0 = unit_tiles(0, 0, M)
+        for t in range(PACK):
+            leave_h(acc0[t], 0, t)
+            pick_tail(damp0, 0, t, 0, M)
+            root_damp(damp0, 0, t)
+            if t > 0:
+                pick_lead(lead0, damp0, 0, t - 1, 0, M)
+                raw = load_w1(1, t - 1)
+                for pair in range(2):
+                    quantise_w1(1, t - 1, pair, round_w1(raw, pair, t == PACK - 1 and pair == 0))
+        pick_lead(lead0, damp0, 0, PACK - 1, 0, M)
+        z_bf0 = round_z(lead0, damp0, 0, 0, M)
+        deal_w4()
+        quantise_z(z_bf0, 0, 0, M)
+
+        acc1 = [[bank(2 * t + s, [P, BANK]) for s in range(2)] for t in range(PACK)]
+        for t in range(PACK):
+            for a in range(K_PASSES):
+                first_pass(acc1[t], 1, t, a)
+
+        out_rows = out_0.rearrange("(g p t) m -> g p t m", p=P, t=PACK)
+        out_words = out_1.rearrange("g p m t -> p g (m t)").bitcast(I32)
+
+        def second_stage(ci, lo, hi):
+            w = hi - lo
+            y_w = held([P, N_GROUPS, w], U32, "y_w%d" % lo)
+            for g in range(N_GROUPS):
+                y = held([P, PACK, w], F32, "y%d_%d" % (g, lo))
+                for half in range(2):
+                    acc = bank(4 * (ci % 2) + 2 * g + half, [P, 2, w])
+                    for tt in range(2):
+                        t = 2 * half + tt
+                        for a in range(H_PASSES):
+                            first = (a * N_GROUPS + g) * PASS + t * P
+                            nc.tensor.matmul_mx(
+                                out=acc[:, tt, :],
+                                lhsT=w4_w[:, first : first + P].bitcast(FP4X4),
+                                lhsT_scale=w4_s[:, first : first + P],
+                                rhs=z_w[a][:, lo:hi].bitcast(FP8X4),
+                                rhs_scale=z_s[a][:, lo:hi],
+                                start=(a == 0),
+                                stop=(a == H_PASSES - 1),
+                            )
+                    nc.scalar.copy(out=y[:, 2 * half : 2 * half + 2, :], in_=acc[:])
+                nc.sync.dma_start(out=out_rows[g][:, :, lo:hi], in_=y[:])
+                y_bf = held([P, w, PACK], BF16, "y_bf%d_%d" % (g, lo))
+                nc.vector.tensor_copy(
+                    y_bf[:].rearrange("p (c i) t -> p c t i", i=4), y[:].rearrange("p t (c i) -> p c t i", i=4)
+                )
+                nc.vector.quantize_mx(
+                    out=y_w[:, g, :].bitcast(FP8X4), scales=y_s[:, g, lo:hi], in_=y_bf[:].rearrange("p m t -> p (m t)")
+                )
+            nc.sync.dma_start(out=out_words[:, :, lo:hi], in_=y_w[:].bitcast(I32))
+
+        pending = None
+        for ci, (lo, hi) in enumerate(CHUNKS):
+            damp1, lead1 = unit_tiles(1, lo, hi)
+            for t in range(PACK):
+                if ci == 0:
+                    leave_h(acc1[t], 1, t)
+                pick_tail(damp1, 1, t, lo, hi)
+                root_damp(damp1, 1, t)
+                if t > 0:
+                    pick_lead(lead1, damp1, 1, t - 1, lo, hi)
+            pick_lead(lead1, damp1, 1, PACK - 1, lo, hi)
+            if pending is not None:
+                second_stage(*pending)
+            quantise_z(round_z(lead1, damp1, 1, lo, hi), 1, lo, hi)
+            pending = (ci, lo, hi)
+        second_stage(*pending)
+        for q in range(QUADS):
+            nc.sync.dma_start(
+                out=out_2[:, 4 * q : 4 * q + 4, :].bitcast(I32).rearrange("g r m -> r g m"),
+                in_=y_s[32 * q : 32 * q + 4].bitcast(I32),
+            )

@@ -27,7 +27,7 @@ QUADS = 4
 LIVE_SPAN = 100
 SCALE_ROW0 = 20
 PAIR = 2
-CHUNKS = ((0, 256), (256, 512))
+CHUNKS = ((0, 256), (256, 384), (384, 512))
 
 
 def tile_list_lead_tail_fouling_kernel(
@@ -53,7 +53,6 @@ def tile_list_lead_tail_fouling_kernel(
         w1_s = {(b, a): held([P, PASS], U8, "w1_s%d%d" % (b, a)) for b in range(H_PASSES) for a in range(K_PASSES)}
         bias = held([P, H_PASSES, PACK], F32, "bias")
         gains = held([P, H_PASSES, PACK], F32, "gains")
-        w4_s_raw = held([P, H_PASSES * N], U8, "w4_s_raw")
         w4_w = held([P, H_PASSES * N], U16, "w4_w")
         w4_s = held([P, H_PASSES * N], U8, "w4_s")
         h = {(b, t): held([P, S], F32, "h%d%d" % (b, t)) for b in range(H_PASSES) for t in range(PACK)}
@@ -83,14 +82,13 @@ def tile_list_lead_tail_fouling_kernel(
             )
             return raw
 
+        for q in range(QUADS):
+            engine = nc.vector if q % 2 == 0 else nc.gpsimd
+            engine.memset(tab_s[32 * q : 32 * q + SCALE_ROW0, :].bitcast(I32), 0)
         for a in range(K_PASSES):
             nc.vector.memset(v_s[a][:].bitcast(I32), 0)
-        nc.gpsimd.memset(w4_s_raw[:].bitcast(I32), 0)
-        for q in range(QUADS):
-            nc.gpsimd.dma_start(
-                out=w4_s_raw[32 * q : 32 * q + 4, :].bitcast(I32).rearrange("r (a n) -> r a n", a=H_PASSES),
-                in_=w4_scales[:, 4 * q : 4 * q + 4, :].bitcast(I32).rearrange("a r n -> r a n"),
-            )
+        nc.gpsimd.dma_start(out=bias[:], in_=b1.rearrange("(b p t) -> p b t", p=P, t=PACK))
+        nc.gpsimd.dma_start(out=gains[:], in_=gain.rearrange("(b p t) -> p b t", p=P, t=PACK))
 
         def round_w1(raw, pair, on_vector):
             grouped = ring.tile([P, PAIR * PASS], BF16, name="w1_bf", align_bytes=64)
@@ -125,19 +123,22 @@ def tile_list_lead_tail_fouling_kernel(
 
         def leave_h(acc, b, t):
             for s in range(S // BANK):
-                nc.scalar.activation(
-                    out=h[b, t][:, BANK * s : BANK * (s + 1)], in_=acc[s][:], func=ACT.Identity, bias=bias[:, b, t : t + 1]
-                )
+                cols = h[b, t][:, BANK * s : BANK * (s + 1)]
+                if (b, t, s) == (0, 0, 1):
+                    nc.vector.tensor_scalar_add(cols, acc[s][:], bias[:, b, t : t + 1])
+                else:
+                    nc.scalar.activation(out=cols, in_=acc[s][:], func=ACT.Identity, bias=bias[:, b, t : t + 1])
 
         tab_w = [load_tab(0)]
         nc.sync.dma_start(offs_sb[:], offs)
         for q in range(QUADS):
-            nc.vector.memset(tab_s[32 * q : 32 * q + SCALE_ROW0, :].bitcast(I32), 0)
             nc.sync.dma_start(
                 out=tab_s[32 * q + SCALE_ROW0 : 32 * (q + 1), :].bitcast(I32),
                 in_=tab_scales[:, 4 * q : 4 * q + 4, :].bitcast(I32),
             )
         tab_w.extend(load_tab(a) for a in range(1, K_PASSES))
+        nc.sync.dma_start(pos2_sb[:], pos2)
+        nc.sync.dma_start(pos1_sb[:], pos1)
         nc.vector.tensor_copy(v_s_all[:], tab_s[:].indirect(offs_sb[:]))
         for a in range(K_PASSES):
             row = SCALE_ROW0 + 4 * a
@@ -147,16 +148,22 @@ def tile_list_lead_tail_fouling_kernel(
         acc0 = [[bank(2 * t + s, [P, BANK]) for s in range(2)] for t in range(PACK)]
         for a in range(K_PASSES):
             raw = load_w1(0, a)
-            halves = [round_w1(raw, pair, pair == 0) for pair in range(2)]
+            halves = [round_w1(raw, pair, pair == 0 and a > 0) for pair in range(2)]
             for pair in range(2):
                 quantise_w1(0, a, pair, halves[pair])
-                for t in range(PAIR * pair, PAIR * (pair + 1)):
-                    first_pass(acc0[t], 0, t, a)
-        nc.sync.dma_start(out=bias[:], in_=b1.rearrange("(b p t) -> p b t", p=P, t=PACK))
-        nc.sync.dma_start(out=gains[:], in_=gain.rearrange("(b p t) -> p b t", p=P, t=PACK))
-        nc.sync.dma_start(pos2_sb[:], pos2)
-        nc.sync.dma_start(pos1_sb[:], pos1)
+        for t in range(PACK):
+            first_pass(acc0[t], 0, t, 0)
+        for t in range(PACK):
+            for a in range(1, K_PASSES):
+                first_pass(acc0[t], 0, t, a)
         w4_w_raw = load_w4()
+        w4_s_raw = landing([P, H_PASSES * N], U8)
+        nc.vector.memset(w4_s_raw[:].bitcast(I32), 0)
+        for q in range(QUADS):
+            nc.sync.dma_start(
+                out=w4_s_raw[32 * q : 32 * q + 4, :].bitcast(I32).rearrange("r (a n) -> r a n", a=H_PASSES),
+                in_=w4_scales[:, 4 * q : 4 * q + 4, :].bitcast(I32).rearrange("a r n -> r a n"),
+            )
 
         def unit_tiles(b, lo, hi):
             w = hi - lo
@@ -197,16 +204,18 @@ def tile_list_lead_tail_fouling_kernel(
             )
 
         damp0, lead0 = unit_tiles(0, 0, M)
+        leave_h(acc0[0], 0, 0)
+        pick_tail(damp0, 0, 0, 0, M)
         for t in range(PACK):
-            leave_h(acc0[t], 0, t)
-            pick_tail(damp0, 0, t, 0, M)
+            if t + 1 < PACK:
+                leave_h(acc0[t + 1], 0, t + 1)
+                pick_tail(damp0, 0, t + 1, 0, M)
             root_damp(damp0, 0, t)
+            pick_lead(lead0, damp0, 0, t, 0, M)
             if t > 0:
-                pick_lead(lead0, damp0, 0, t - 1, 0, M)
                 raw = load_w1(1, t - 1)
                 for pair in range(2):
-                    quantise_w1(1, t - 1, pair, round_w1(raw, pair, t == PACK - 1 and pair == 0))
-        pick_lead(lead0, damp0, 0, PACK - 1, 0, M)
+                    quantise_w1(1, t - 1, pair, round_w1(raw, pair, pair == 0))
         z_bf0 = round_z(lead0, damp0, 0, 0, M)
         deal_w4()
         quantise_z(z_bf0, 0, 0, M)
@@ -218,56 +227,85 @@ def tile_list_lead_tail_fouling_kernel(
 
         out_rows = out_0.rearrange("(g p t) m -> g p t m", p=P, t=PACK)
         out_words = out_1.rearrange("g p m t -> p g (m t)").bitcast(I32)
+        y_acc = {}
 
-        def second_stage(ci, lo, hi):
+        def second_pass(a, lo, hi):
             w = hi - lo
-            y_w = held([P, N_GROUPS, w], U32, "y_w%d" % lo)
+            per_bank = BANK // w
             for g in range(N_GROUPS):
-                y = held([P, PACK, w], F32, "y%d_%d" % (g, lo))
-                for half in range(2):
-                    acc = bank(4 * (ci % 2) + 2 * g + half, [P, 2, w])
-                    for tt in range(2):
-                        t = 2 * half + tt
-                        for a in range(H_PASSES):
-                            first = (a * N_GROUPS + g) * PASS + t * P
-                            nc.tensor.matmul_mx(
-                                out=acc[:, tt, :],
-                                lhsT=w4_w[:, first : first + P].bitcast(FP4X4),
-                                lhsT_scale=w4_s[:, first : first + P],
-                                rhs=z_w[a][:, lo:hi].bitcast(FP8X4),
-                                rhs_scale=z_s[a][:, lo:hi],
-                                start=(a == 0),
-                                stop=(a == H_PASSES - 1),
-                            )
-                    nc.scalar.copy(out=y[:, 2 * half : 2 * half + 2, :], in_=acc[:])
-                nc.sync.dma_start(out=out_rows[g][:, :, lo:hi], in_=y[:])
-                y_bf = held([P, w, PACK], BF16, "y_bf%d_%d" % (g, lo))
-                nc.vector.tensor_copy(
-                    y_bf[:].rearrange("p (c i) t -> p c t i", i=4), y[:].rearrange("p t (c i) -> p c t i", i=4)
-                )
+                for t0 in range(0, PACK, per_bank):
+                    if a == 0:
+                        y_acc[lo, g, t0] = bank(len(y_acc), [P, per_bank, w])
+                    for tt in range(per_bank):
+                        first = (a * N_GROUPS + g) * PASS + (t0 + tt) * P
+                        nc.tensor.matmul_mx(
+                            out=y_acc[lo, g, t0][:, tt, :],
+                            lhsT=w4_w[:, first : first + P].bitcast(FP4X4),
+                            lhsT_scale=w4_s[:, first : first + P],
+                            rhs=z_w[a][:, lo:hi].bitcast(FP8X4),
+                            rhs_scale=z_s[a][:, lo:hi],
+                            start=(a == 0 and tt == 0),
+                            stop=(a == H_PASSES - 1 and tt == per_bank - 1),
+                        )
+
+        def hand_out(lo, hi):
+            w = hi - lo
+            per_bank = BANK // w
+            y_w = held([P, N_GROUPS, w], U32, "y_w%d" % lo)
+            y = [held([P, PACK, w], F32, "y%d_%d" % (g, lo)) for g in range(N_GROUPS)]
+            y_bf = [held([P, w, PACK], BF16, "y_bf%d_%d" % (g, lo)) for g in range(N_GROUPS)]
+
+            def leave_y(g):
+                for t0 in range(0, PACK, per_bank):
+                    nc.scalar.copy(out=y[g][:, t0 : t0 + per_bank, :], in_=y_acc[lo, g, t0][:])
+                nc.sync.dma_start(out=out_rows[g][:, :, lo:hi], in_=y[g][:])
+
+            def quantise_y(g):
                 nc.vector.quantize_mx(
-                    out=y_w[:, g, :].bitcast(FP8X4), scales=y_s[:, g, lo:hi], in_=y_bf[:].rearrange("p m t -> p (m t)")
+                    out=y_w[:, g, :].bitcast(FP8X4), scales=y_s[:, g, lo:hi], in_=y_bf[g][:].rearrange("p m t -> p (m t)")
                 )
+
+            if per_bank == PACK:
+                for g in range(N_GROUPS):
+                    leave_y(g)
+                    other = N_GROUPS - 1 - g
+                    nc.vector.tensor_copy(y_bf[other][:], y_acc[lo, other, 0][:].rearrange("p t m -> p m t"))
+                for g in reversed(range(N_GROUPS)):
+                    quantise_y(g)
+            else:
+                for g in range(N_GROUPS):
+                    leave_y(g)
+                    nc.scalar.copy(
+                        out=y_bf[g][:].rearrange("p (c i) t -> p c t i", i=4), in_=y[g][:].rearrange("p t (c i) -> p c t i", i=4)
+                    )
+                    quantise_y(g)
             nc.sync.dma_start(out=out_words[:, :, lo:hi], in_=y_w[:].bitcast(I32))
 
         pending = None
         for ci, (lo, hi) in enumerate(CHUNKS):
             damp1, lead1 = unit_tiles(1, lo, hi)
+            if ci == 0:
+                leave_h(acc1[0], 1, 0)
+            pick_tail(damp1, 1, 0, lo, hi)
             for t in range(PACK):
-                if ci == 0:
-                    leave_h(acc1[t], 1, t)
-                pick_tail(damp1, 1, t, lo, hi)
+                if t + 1 < PACK:
+                    if ci == 0:
+                        leave_h(acc1[t + 1], 1, t + 1)
+                    pick_tail(damp1, 1, t + 1, lo, hi)
                 root_damp(damp1, 1, t)
-                if t > 0:
-                    pick_lead(lead1, damp1, 1, t - 1, lo, hi)
-            pick_lead(lead1, damp1, 1, PACK - 1, lo, hi)
-            if pending is not None:
-                second_stage(*pending)
+                pick_lead(lead1, damp1, 1, t, lo, hi)
+            if ci == 0:
+                for chunk in CHUNKS:
+                    second_pass(0, *chunk)
             quantise_z(round_z(lead1, damp1, 1, lo, hi), 1, lo, hi)
-            pending = (ci, lo, hi)
-        second_stage(*pending)
+            second_pass(1, lo, hi)
+            if pending is not None:
+                hand_out(*pending)
+            pending = (lo, hi)
+        hand_out(*pending)
         for q in range(QUADS):
-            nc.sync.dma_start(
+            queue = nc.sync if q % 2 == 0 else nc.scalar
+            queue.dma_start(
                 out=out_2[:, 4 * q : 4 * q + 4, :].bitcast(I32).rearrange("g r m -> r g m"),
                 in_=y_s[32 * q : 32 * q + 4].bitcast(I32),
             )

@@ -24,8 +24,7 @@ K_PASSES = K // PASS
 H_PASSES = H // PASS
 N_GROUPS = N // PASS
 QUADS = 4
-LIVE_SPAN = 100
-SCALE_ROW0 = 20
+SCALE_ROWS = 16
 PAIR = 2
 CHUNKS = ((0, 256), (256, 384), (384, 512))
 
@@ -82,9 +81,8 @@ def tile_list_lead_tail_fouling_kernel(
             )
             return raw
 
-        for q in range(QUADS):
-            engine = nc.vector if q % 2 == 0 else nc.gpsimd
-            engine.memset(tab_s[32 * q : 32 * q + SCALE_ROW0, :].bitcast(I32), 0)
+        nc.vector.memset(tab_s[0:SCALE_ROWS, :].bitcast(I32), 0)
+        nc.gpsimd.memset(tab_s[P // 2 : P, :].bitcast(I32), 0)
         for a in range(K_PASSES):
             nc.vector.memset(v_s[a][:].bitcast(I32), 0)
         nc.gpsimd.dma_start(out=bias[:], in_=b1.rearrange("(b p t) -> p b t", p=P, t=PACK))
@@ -129,20 +127,20 @@ def tile_list_lead_tail_fouling_kernel(
                 else:
                     nc.scalar.activation(out=cols, in_=acc[s][:], func=ACT.Identity, bias=bias[:, b, t : t + 1])
 
-        tab_w = [load_tab(0)]
         nc.sync.dma_start(offs_sb[:], offs)
-        for q in range(QUADS):
+        for a in range(K_PASSES):
             nc.sync.dma_start(
-                out=tab_s[32 * q + SCALE_ROW0 : 32 * (q + 1), :].bitcast(I32),
-                in_=tab_scales[:, 4 * q : 4 * q + 4, :].bitcast(I32),
+                out=tab_s[SCALE_ROWS * (a + 1) : SCALE_ROWS * (a + 2), :].bitcast(I32), in_=tab_scales[a].bitcast(I32)
             )
-        tab_w.extend(load_tab(a) for a in range(1, K_PASSES))
+        tab_w = [load_tab(0), load_tab(1)]
         nc.sync.dma_start(pos2_sb[:], pos2)
         nc.sync.dma_start(pos1_sb[:], pos1)
+        tab_w.append(load_tab(2))
         nc.vector.tensor_copy(v_s_all[:], tab_s[:].indirect(offs_sb[:]))
         for a in range(K_PASSES):
-            row = SCALE_ROW0 + 4 * a
-            nc.scalar.dma_start(out=v_s[a][0:LIVE_SPAN, :].bitcast(I32), in_=v_s_all[row : row + LIVE_SPAN, :].bitcast(I32))
+            for q in range(QUADS):
+                row = SCALE_ROWS * (a + 1) + 4 * q
+                nc.scalar.dma_start(out=v_s[a][32 * q : 32 * q + 4, :].bitcast(I32), in_=v_s_all[row : row + 4, :].bitcast(I32))
         for a in range(K_PASSES):
             nc.vector.tensor_copy(v_w[a][:], tab_w[a][:].indirect(offs_sb[:]))
         acc0 = [[bank(2 * t + s, [P, BANK]) for s in range(2)] for t in range(PACK)]
@@ -183,9 +181,9 @@ def tile_list_lead_tail_fouling_kernel(
         def round_z(lead, damp, b, lo, hi):
             z_bf = held([P, hi - lo, PACK], BF16, "z_bf%d_%d" % (b, lo))
             nc.vector.tensor_tensor(
-                z_bf[:].rearrange("p (c i) t -> p c t i", i=4),
-                lead[:].rearrange("p t (c i) -> p c t i", i=4),
-                damp[:].rearrange("p t (c i) -> p c t i", i=4),
+                z_bf[:].rearrange("p (c i) t -> p c t i", i=2),
+                lead[:].rearrange("p t (c i) -> p c t i", i=2),
+                damp[:].rearrange("p t (c i) -> p c t i", i=2),
                 ALU.mult,
             )
             return z_bf
@@ -276,7 +274,7 @@ def tile_list_lead_tail_fouling_kernel(
                 for g in range(N_GROUPS):
                     leave_y(g)
                     nc.scalar.copy(
-                        out=y_bf[g][:].rearrange("p (c i) t -> p c t i", i=4), in_=y[g][:].rearrange("p t (c i) -> p c t i", i=4)
+                        out=y_bf[g][:].rearrange("p (c i) t -> p c t i", i=2), in_=y[g][:].rearrange("p t (c i) -> p c t i", i=2)
                     )
                     quantise_y(g)
             nc.sync.dma_start(out=out_words[:, :, lo:hi], in_=y_w[:].bitcast(I32))

@@ -26,7 +26,7 @@ N_GROUPS = N // PASS
 QUADS = 4
 SCALE_ROWS = 16
 PAIR = 2
-CHUNKS = ((0, 256), (256, 384), (384, 512))
+CHUNKS = ((0, 256), (256, 512))
 
 
 def tile_list_lead_tail_fouling_kernel(
@@ -146,15 +146,12 @@ def tile_list_lead_tail_fouling_kernel(
         acc0 = [[bank(2 * t + s, [P, BANK]) for s in range(2)] for t in range(PACK)]
         for a in range(K_PASSES):
             raw = load_w1(0, a)
-            halves = [round_w1(raw, pair, pair == 0 and a > 0) for pair in range(2)]
+            halves = [round_w1(raw, pair, pair == 0) for pair in range(2)]
             for pair in range(2):
                 quantise_w1(0, a, pair, halves[pair])
         for t in range(PACK):
-            first_pass(acc0[t], 0, t, 0)
-        for t in range(PACK):
-            for a in range(1, K_PASSES):
+            for a in range(K_PASSES):
                 first_pass(acc0[t], 0, t, a)
-        w4_w_raw = load_w4()
         w4_s_raw = landing([P, H_PASSES * N], U8)
         nc.vector.memset(w4_s_raw[:].bitcast(I32), 0)
         for q in range(QUADS):
@@ -162,6 +159,8 @@ def tile_list_lead_tail_fouling_kernel(
                 out=w4_s_raw[32 * q : 32 * q + 4, :].bitcast(I32).rearrange("r (a n) -> r a n", a=H_PASSES),
                 in_=w4_scales[:, 4 * q : 4 * q + 4, :].bitcast(I32).rearrange("a r n -> r a n"),
             )
+
+        w4_w_raw = load_w4()
 
         def unit_tiles(b, lo, hi):
             w = hi - lo
@@ -174,17 +173,15 @@ def tile_list_lead_tail_fouling_kernel(
         def root_damp(damp, b, t):
             nc.scalar.activation(out=damp[:, t, :], in_=damp[:, t, :], func=ACT.Square, scale=gains[:, b, t : t + 1])
             nc.scalar.activation(out=damp[:, t, :], in_=damp[:, t, :], func=ACT.Abs_reciprocal_sqrt, bias=1.0)
+            nc.scalar.activation(out=damp[:, t, :], in_=damp[:, t, :], func=ACT.Square)
 
         def pick_lead(lead, damp, b, t, lo, hi):
             nc.vector.tensor_tensor(lead[:, t, :], h[b, t][:].indirect(pos1_sb[:, lo // 16 : hi // 16]), damp[:, t, :], ALU.mult)
 
         def round_z(lead, damp, b, lo, hi):
             z_bf = held([P, hi - lo, PACK], BF16, "z_bf%d_%d" % (b, lo))
-            nc.vector.tensor_tensor(
-                z_bf[:].rearrange("p (c i) t -> p c t i", i=2),
-                lead[:].rearrange("p t (c i) -> p c t i", i=2),
-                damp[:].rearrange("p t (c i) -> p c t i", i=2),
-                ALU.mult,
+            nc.vector.tensor_copy(
+                z_bf[:].rearrange("p (c i) t -> p c t i", i=2), lead[:].rearrange("p t (c i) -> p c t i", i=2)
             )
             return z_bf
 
@@ -194,7 +191,7 @@ def tile_list_lead_tail_fouling_kernel(
             )
 
         def deal_w4():
-            nc.vector.tensor_copy(
+            nc.scalar.copy(
                 w4_w[:].rearrange("p (g t m) -> p g t m", t=PACK, m=P), w4_w_raw[:].rearrange("p (g m t) -> p g t m", t=PACK, m=P)
             )
             nc.vector.tensor_copy(
@@ -213,7 +210,7 @@ def tile_list_lead_tail_fouling_kernel(
             if t > 0:
                 raw = load_w1(1, t - 1)
                 for pair in range(2):
-                    quantise_w1(1, t - 1, pair, round_w1(raw, pair, pair == 0))
+                    quantise_w1(1, t - 1, pair, round_w1(raw, pair, pair == 0 or t == PACK - 1))
         z_bf0 = round_z(lead0, damp0, 0, 0, M)
         deal_w4()
         quantise_z(z_bf0, 0, 0, M)
@@ -263,20 +260,12 @@ def tile_list_lead_tail_fouling_kernel(
                     out=y_w[:, g, :].bitcast(FP8X4), scales=y_s[:, g, lo:hi], in_=y_bf[g][:].rearrange("p m t -> p (m t)")
                 )
 
-            if per_bank == PACK:
-                for g in range(N_GROUPS):
-                    leave_y(g)
-                    other = N_GROUPS - 1 - g
-                    nc.vector.tensor_copy(y_bf[other][:], y_acc[lo, other, 0][:].rearrange("p t m -> p m t"))
-                for g in reversed(range(N_GROUPS)):
-                    quantise_y(g)
-            else:
-                for g in range(N_GROUPS):
-                    leave_y(g)
-                    nc.scalar.copy(
-                        out=y_bf[g][:].rearrange("p (c i) t -> p c t i", i=2), in_=y[g][:].rearrange("p t (c i) -> p c t i", i=2)
-                    )
-                    quantise_y(g)
+            for g in range(N_GROUPS):
+                leave_y(g)
+                nc.vector.tensor_copy(
+                    y_bf[g][:].rearrange("p (c i) t -> p c t i", i=2), y[g][:].rearrange("p t (c i) -> p c t i", i=2)
+                )
+                quantise_y(g)
             nc.sync.dma_start(out=out_words[:, :, lo:hi], in_=y_w[:].bitcast(I32))
 
         pending = None

@@ -59,6 +59,9 @@ def tile_list_lead_tail_fouling_kernel(
         z_s = [held([P, M], U8, "z_s%d" % b) for b in range(H_PASSES)]
         y_s = held([P, N_GROUPS, M], U8, "y_s")
 
+        warm = held([P, 8], F32, "warm")
+        nc.vector.memset(warm[:, 0:4], 1.0)
+        nc.scalar.activation(out=warm[:, 4:8], in_=warm[:, 0:4], func=ACT.Abs_reciprocal_sqrt)
         def landing(shape, dtype):
             return ring.tile(shape, dtype, name="landing", align_bytes=64)
 

from contextlib import ExitStack

import concourse.mybir as mybir

K, H, N, T, S, M = 1536, 1024, 1024, 4096, 1024, 512
FLOPS = 2 * K * H * S + 2 * H * N * M

F32 = mybir.dt.float32
BF16 = mybir.dt.bfloat16
I32 = mybir.dt.int32
U32 = mybir.dt.uint32
U16 = mybir.dt.uint16
U8 = mybir.dt.uint8
FP8X4 = mybir.dt.float8_e4m3fn_x4
FP4X4 = mybir.dt.float4_e2m1fn_x4
ACT = mybir.ActivationFunctionType
ALU = mybir.AluOpType

P = 128
PACK = 4
PASS = P * PACK
BANK = 512
K_PASSES = K // PASS
H_PASSES = H // PASS
N_GROUPS = N // PASS
QUADS = 4
SCALE_ROWS = 16
PAIR = 2
CHUNKS = ((0, 256), (256, 512))


def tile_list_lead_tail_fouling_kernel(
    tc, tab_words, tab_scales, offs, pos1, pos2, w1, b1, gain, w4_words, w4_scales, out_0, out_1, out_2
):
    nc = tc.nc
    with ExitStack() as ctx:
        keep = ctx.enter_context(tc.tile_pool(name="keep", bufs=1))
        ring = ctx.enter_context(tc.tile_pool(name="ring", bufs=4))
        psum = ctx.enter_context(tc.psum_pool(name="psum", bufs=1))

        def held(shape, dtype, name):
            return keep.tile(shape, dtype, name=name, align_bytes=64)

        offs_sb = held([P, S // 16], U16, "offs")
        pos1_sb = held([P, M // 16], U16, "pos1")
        pos2_sb = held([P, M // 16], U16, "pos2")
        tab_s = held([P, T], U8, "tab_s")
        v_w = [held([P, S], U16, "v_w%d" % a) for a in range(K_PASSES)]
        v_s_all = held([P, S], U8, "v_s_all")
        v_s = [held([P, S], U8, "v_s%d" % a) for a in range(K_PASSES)]
        w1_w = {(b, a): held([P, PASS], U32, "w1_w%d%d" % (b, a)) for b in range(H_PASSES) for a in range(K_PASSES)}
        w1_s = {(b, a): held([P, PASS], U8, "w1_s%d%d" % (b, a)) for b in range(H_PASSES) for a in range(K_PASSES)}
        bias = held([P, H_PASSES, PACK], F32, "bias")
        gains = held([P, H_PASSES, PACK], F32, "gains")
        w4_w = held([P, H_PASSES * N], U16, "w4_w")
        w4_s = held([P, H_PASSES * N], U8, "w4_s")
        h = {(b, t): held([P, S], F32, "h%d%d" % (b, t)) for b in range(H_PASSES) for t in range(PACK)}
        z_w = [held([P, M], U32, "z_w%d" % b) for b in range(H_PASSES)]
        z_s = [held([P, M], U8, "z_s%d" % b) for b in range(H_PASSES)]
        y_s = held([P, N_GROUPS, M], U8, "y_s")

        warm = held([P, 8], F32, "warm")
        nc.vector.memset(warm[:, 0:4], 1.0)
        nc.scalar.activation(out=warm[:, 4:8], in_=warm[:, 0:4], func=ACT.Abs_reciprocal_sqrt)
        def landing(shape, dtype):
            return ring.tile(shape, dtype, name="landing", align_bytes=64)

        def load_tab(a):
            words = landing([P, T], U16)
            nc.sync.dma_start(out=words[:].bitcast(I32), in_=tab_words[a].bitcast(I32))
            return words

        def load_w1(b, a):
            raw = landing([P, PACK, PASS], F32)
            rows = w1[PASS * a : PASS * (a + 1), PASS * b : PASS * (b + 1)]
            nc.sync.dma_start(out=raw[:], in_=rows.rearrange("(p j) c -> p j c", j=PACK))
            return raw

        def load_w4():
            raw = landing([P, H_PASSES * N], U16)
            nc.sync.dma_start(
                out=raw[:].bitcast(I32).rearrange("p (a n) -> p a n", a=H_PASSES),
                in_=w4_words.bitcast(I32).rearrange("a p n -> p a n"),
            )
            return raw

        nc.vector.memset(tab_s[0:SCALE_ROWS, :].bitcast(I32), 0)
        nc.gpsimd.memset(tab_s[P // 2 : P, :].bitcast(I32), 0)
        for a in range(K_PASSES):
            nc.vector.memset(v_s[a][:].bitcast(I32), 0)
        nc.gpsimd.dma_start(out=bias[:], in_=b1.rearrange("(b p t) -> p b t", p=P, t=PACK))
        nc.gpsimd.dma_start(out=gains[:], in_=gain.rearrange("(b p t) -> p b t", p=P, t=PACK))

        def round_w1(raw, pair, on_vector):
            grouped = ring.tile([P, PAIR * PASS], BF16, name="w1_bf", align_bytes=64)
            dst = grouped[:].rearrange("p (t m j) -> p m j t", t=PAIR, j=PACK)
            src = raw[:].rearrange("p j (m t) -> p m j t", t=PACK)[:, :, :, PAIR * pair : PAIR * (pair + 1)]
            if on_vector:
                nc.vector.tensor_copy(dst, src)
            else:
                nc.scalar.activation(out=dst, in_=src, func=ACT.Copy)
            return grouped

        def quantise_w1(b, a, pair, grouped):
            cols = slice(PAIR * P * pair, PAIR * P * (pair + 1))
            nc.vector.quantize_mx(out=w1_w[b, a][:, cols].bitcast(FP8X4), scales=w1_s[b, a][:, cols], in_=grouped[:])

        def bank(i, shape):
            return psum.tile(shape, F32, name="bank%d" % i)

        def first_pass(acc, b, t, a):
            for s in range(S // BANK):
                rows = slice(P * t, P * (t + 1))
                cols = slice(BANK * s, BANK * (s + 1))
                nc.tensor.matmul_mx(
                    out=acc[s][:],
                    lhsT=w1_w[b, a][:, rows].bitcast(FP8X4),
                    lhsT_scale=w1_s[b, a][:, rows],
                    rhs=v_w[a][:, cols].bitcast(FP4X4),
                    rhs_scale=v_s[a][:, cols],
                    start=(a == 0),
                    stop=(a == K_PASSES - 1),
                )

        def leave_h(acc, b, t):
            for s in range(S // BANK):
                cols = h[b, t][:, BANK * s : BANK * (s + 1)]
                if (b, t, s) == (0, 0, 1):
                    nc.vector.tensor_scalar_add(cols, acc[s][:], bias[:, b, t : t + 1])
                else:
                    nc.scalar.activation(out=cols, in_=acc[s][:], func=ACT.Identity, bias=bias[:, b, t : t + 1])

        nc.sync.dma_start(offs_sb[:], offs)
        for a in range(K_PASSES):
            nc.sync.dma_start(
                out=tab_s[SCALE_ROWS * (a + 1) : SCALE_ROWS * (a + 2), :].bitcast(I32), in_=tab_scales[a].bitcast(I32)
            )
        tab_w = [load_tab(0), load_tab(1)]
        nc.sync.dma_start(pos2_sb[:], pos2)
        nc.sync.dma_start(pos1_sb[:], pos1)
        tab_w.append(load_tab(2))
        nc.vector.tensor_copy(v_s_all[:], tab_s[:].indirect(offs_sb[:]))
        for a in range(K_PASSES):
            for q in range(QUADS):
                row = SCALE_ROWS * (a + 1) + 4 * q
                nc.scalar.dma_start(out=v_s[a][32 * q : 32 * q + 4, :].bitcast(I32), in_=v_s_all[row : row + 4, :].bitcast(I32))
        for a in range(K_PASSES):
            nc.vector.tensor_copy(v_w[a][:], tab_w[a][:].indirect(offs_sb[:]))
        acc0 = [[bank(2 * t + s, [P, BANK]) for s in range(2)] for t in range(PACK)]
        for a in range(K_PASSES):
            raw = load_w1(0, a)
            halves = [round_w1(raw, pair, pair == 0) for pair in range(2)]
            for pair in range(2):
                quantise_w1(0, a, pair, halves[pair])
        for t in range(PACK):
            for a in range(K_PASSES):
                first_pass(acc0[t], 0, t, a)
        w4_s_raw = landing([P, H_PASSES * N], U8)
        nc.vector.memset(w4_s_raw[:].bitcast(I32), 0)
        for q in range(QUADS):
            nc.sync.dma_start(
                out=w4_s_raw[32 * q : 32 * q + 4, :].bitcast(I32).rearrange("r (a n) -> r a n", a=H_PASSES),
                in_=w4_scales[:, 4 * q : 4 * q + 4, :].bitcast(I32).rearrange("a r n -> r a n"),
            )

        w4_w_raw = load_w4()

        def unit_tiles(b, lo, hi):
            w = hi - lo
            name = "%d_%d" % (b, lo)
            return held([P, PACK, w], F32, "damp" + name), held([P, PACK, w], F32, "lead" + name)

        def pick_tail(damp, b, t, lo, hi):
            nc.vector.tensor_copy(damp[:, t, :], h[b, t][:].indirect(pos2_sb[:, lo // 16 : hi // 16]))

        def root_damp(damp, b, t):
            nc.scalar.activation(out=damp[:, t, :], in_=damp[:, t, :], func=ACT.Square, scale=gains[:, b, t : t + 1])
            nc.scalar.activation(out=damp[:, t, :], in_=damp[:, t, :], func=ACT.Abs_reciprocal_sqrt, bias=1.0)
            nc.scalar.activation(out=damp[:, t, :], in_=damp[:, t, :], func=ACT.Square)

        def pick_lead(lead, damp, b, t, lo, hi):
            nc.vector.tensor_tensor(lead[:, t, :], h[b, t][:].indirect(pos1_sb[:, lo // 16 : hi // 16]), damp[:, t, :], ALU.mult)

        def round_z(lead, damp, b, lo, hi):
            z_bf = held([P, hi - lo, PACK], BF16, "z_bf%d_%d" % (b, lo))
            nc.vector.tensor_copy(
                z_bf[:].rearrange("p (c i) t -> p c t i", i=2), lead[:].rearrange("p t (c i) -> p c t i", i=2)
            )
            return z_bf

        def quantise_z(z_bf, b, lo, hi):
            nc.vector.quantize_mx(
                out=z_w[b][:, lo:hi].bitcast(FP8X4), scales=z_s[b][:, lo:hi], in_=z_bf[:].rearrange("p m t -> p (m t)")
            )

        def deal_w4():
            nc.scalar.copy(
                w4_w[:].rearrange("p (g t m) -> p g t m", t=PACK, m=P), w4_w_raw[:].rearrange("p (g m t) -> p g t m", t=PACK, m=P)
            )
            nc.vector.tensor_copy(
                w4_s[:].rearrange("p (g t m) -> p g t m", t=PACK, m=P), w4_s_raw[:].rearrange("p (g m t) -> p g t m", t=PACK, m=P)
            )

        damp0, lead0 = unit_tiles(0, 0, M)
        leave_h(acc0[0], 0, 0)
        pick_tail(damp0, 0, 0, 0, M)
        for t in range(PACK):
            if t + 1 < PACK:
                leave_h(acc0[t + 1], 0, t + 1)
                pick_tail(damp0, 0, t + 1, 0, M)
            root_damp(damp0, 0, t)
            pick_lead(lead0, damp0, 0, t, 0, M)
            if t > 0:
                raw = load_w1(1, t - 1)
                for pair in range(2):
                    quantise_w1(1, t - 1, pair, round_w1(raw, pair, pair == 0 or t == PACK - 1))
        z_bf0 = round_z(lead0, damp0, 0, 0, M)
        deal_w4()
        quantise_z(z_bf0, 0, 0, M)

        acc1 = [[bank(2 * t + s, [P, BANK]) for s in range(2)] for t in range(PACK)]
        for t in range(PACK):
            for a in range(K_PASSES):
                first_pass(acc1[t], 1, t, a)

        out_rows = out_0.rearrange("(g p t) m -> g p t m", p=P, t=PACK)
        out_words = out_1.rearrange("g p m t -> p g (m t)").bitcast(I32)
        y_acc = {}

        def second_pass(a, lo, hi):
            w = hi - lo
            per_bank = BANK // w
            for g in range(N_GROUPS):
                for t0 in range(0, PACK, per_bank):
                    if a == 0:
                        y_acc[lo, g, t0] = bank(len(y_acc), [P, per_bank, w])
                    for tt in range(per_bank):
                        first = (a * N_GROUPS + g) * PASS + (t0 + tt) * P
                        nc.tensor.matmul_mx(
                            out=y_acc[lo, g, t0][:, tt, :],
                            lhsT=w4_w[:, first : first + P].bitcast(FP4X4),
                            lhsT_scale=w4_s[:, first : first + P],
                            rhs=z_w[a][:, lo:hi].bitcast(FP8X4),
                            rhs_scale=z_s[a][:, lo:hi],
                            start=(a == 0 and tt == 0),
                            stop=(a == H_PASSES - 1 and tt == per_bank - 1),
                        )

        def hand_out(lo, hi):
            w = hi - lo
            per_bank = BANK // w
            y_w = held([P, N_GROUPS, w], U32, "y_w%d" % lo)
            y = [held([P, PACK, w], F32, "y%d_%d" % (g, lo)) for g in range(N_GROUPS)]
            y_bf = [held([P, w, PACK], BF16, "y_bf%d_%d" % (g, lo)) for g in range(N_GROUPS)]

            def leave_y(g):
                for t0 in range(0, PACK, per_bank):
                    nc.scalar.copy(out=y[g][:, t0 : t0 + per_bank, :], in_=y_acc[lo, g, t0][:])
                nc.sync.dma_start(out=out_rows[g][:, :, lo:hi], in_=y[g][:])

            def quantise_y(g):
                nc.vector.quantize_mx(
                    out=y_w[:, g, :].bitcast(FP8X4), scales=y_s[:, g, lo:hi], in_=y_bf[g][:].rearrange("p m t -> p (m t)")
                )

            for g in range(N_GROUPS):
                leave_y(g)
                nc.vector.tensor_copy(
                    y_bf[g][:].rearrange("p (c i) t -> p c t i", i=2), y[g][:].rearrange("p t (c i) -> p c t i", i=2)
                )
                quantise_y(g)
            nc.sync.dma_start(out=out_words[:, :, lo:hi], in_=y_w[:].bitcast(I32))

        pending = None
        for ci, (lo, hi) in enumerate(CHUNKS):
            damp1, lead1 = unit_tiles(1, lo, hi)
            if ci == 0:
                leave_h(acc1[0], 1, 0)
            pick_tail(damp1, 1, 0, lo, hi)
            for t in range(PACK):
                if t + 1 < PACK:
                    if ci == 0:
                        leave_h(acc1[t + 1], 1, t + 1)
                    pick_tail(damp1, 1, t + 1, lo, hi)
                root_damp(damp1, 1, t)
                pick_lead(lead1, damp1, 1, t, lo, hi)
            if ci == 0:
                for chunk in CHUNKS:
                    second_pass(0, *chunk)
            quantise_z(round_z(lead1, damp1, 1, lo, hi), 1, lo, hi)
            second_pass(1, lo, hi)
            if pending is not None:
                hand_out(*pending)
            pending = (lo, hi)
        hand_out(*pending)
        for q in range(QUADS):
            queue = nc.sync if q % 2 == 0 else nc.scalar
            queue.dma_start(
                out=out_2[:, 4 * q : 4 * q + 4, :].bitcast(I32).rearrange("g r m -> r g m"),
                in_=y_s[32 * q : 32 * q + 4].bitcast(I32),
            )
